import numpy as np
import ml_dtypes


def mxq(x, axis, fmt="e4m3"):
    dtype, down = {"e4m3": (ml_dtypes.float8_e4m3fn, 7), "e5m2": (ml_dtypes.float8_e5m2, 14)}[fmt]
    v = np.moveaxis(np.asarray(x, np.float32).astype(ml_dtypes.bfloat16).astype(np.float64), axis, -1)
    blocks = v.reshape(v.shape[:-1] + (-1, 32))
    amax = np.abs(blocks).max(-1, keepdims=True)
    byte = np.maximum(np.where(amax > 0, np.frexp(amax)[1] - 1 + 127, 0) - down, 1)
    scale = np.exp2(byte - 127.0)
    codes = (blocks / scale).astype(np.float32).astype(dtype).astype(np.float64)
    return np.moveaxis((codes * scale).reshape(v.shape), -1, axis)


WIDE = False


def mx_kscale(k):
    if not WIDE:
        return np.ones(k)
    levels = np.array([10, -10, 5, -5, 0])
    if k % 512:
        return np.exp2(np.random.permutation(np.resize(levels, k // 32))).repeat(32)
    a = np.empty((k // 512, 16))
    for p in range(k // 512):
        a[p, :8] = np.random.permutation(np.resize(levels, 8))
        for g in range(8):
            far = levels[np.abs(levels - a[p, g]) >= 10]
            a[p, g + 8] = far[np.random.randint(len(far))]
    return np.exp2(a.ravel()).repeat(32)


def f64(x):
    return np.asarray(x).astype(np.float64)


def striped(idx):
    return np.tile(idx.reshape(-1, 16).T, (8, 1)).astype(np.uint16)


def unstriped(offs):
    return offs[:16].T.reshape(-1).astype(np.int64)


def striped8(idx):
    return np.concatenate([x.reshape(-1, 16).T for x in idx]).astype(np.uint16)


def runs(offs, k):
    lists = np.stack([offs[16 * r : 16 * r + 16].T.reshape(-1) for r in range(8)]).astype(np.int64)
    return lists[np.arange(k) % 512 // 64]


def pack_weight(w):
    k, n = w.shape
    w = f64(np.asarray(w, np.float32).astype(ml_dtypes.bfloat16)).reshape(k // 32, 32, n)
    amax = np.abs(w).max(1)
    byte = np.clip(np.where(amax > 0, np.frexp(amax)[1] - 1 + 127 - 7, 1), 1, 254)
    scaled = (w * np.exp2(127.0 - byte)[:, None, :]).reshape(k, n).astype(np.float32)
    words = np.ascontiguousarray(scaled.reshape(k // 512, 128, 4, n).transpose(0, 1, 3, 2)).astype(ml_dtypes.float8_e4m3fn).view(np.uint8)
    return words, np.ascontiguousarray(byte.astype(np.uint8).reshape(k // 512, 16, n))


def unpack_weight(words, scales):
    g, p, n, _ = words.shape
    vals = np.ascontiguousarray(words).view(ml_dtypes.float8_e4m3fn).astype(np.float64) * np.repeat(np.exp2(scales.astype(np.float64) - 127.0), 8, axis=1)[..., None]
    return vals.transpose(0, 1, 3, 2).reshape(g * 512, n)

def planes(y):
    n, m = y.shape
    v = y.astype(np.float32).astype(ml_dtypes.bfloat16).astype(np.float64).reshape(n // 32, 32, m)
    top = np.abs(v).max(1)
    byte = np.clip(np.where(top > 0, np.frexp(top)[1] - 1 + 127 - 7, 1), 1, 254)
    codes = (v * np.exp2(127.0 - byte)[:, None, :]).reshape(n, m).astype(np.float32).astype(ml_dtypes.float8_e4m3fn).view(np.uint8)
    words = codes.reshape(n // 512, 128, 4, m).transpose(0, 1, 3, 2)
    return np.ascontiguousarray(words), np.ascontiguousarray(byte.astype(np.uint8).reshape(n // 512, 16, m))


K, T, S, N, H, U = 512, 2048, 512, 512, 512, 1024


def setup_inputs():
    n = np.random.standard_normal
    s = mx_kscale(K)[:, None]
    u = mx_kscale(S)
    packed_xT = pack_weight(n((K, T)) * s)
    packed_w1 = pack_weight(n((S, N)) / np.sqrt(S) / u[:, None])
    return {
        "x_words": packed_xT[0],
        "x_scales": packed_xT[1],
        "wa": (n((K, H)) / np.sqrt(K) / s).astype(np.float32),
        "gt": (np.random.uniform(0.5, 1.5, (S, 1)) * u[:, None]).astype(np.float32),
        "w1_words": packed_w1[0],
        "w1_scales": packed_w1[1],
        "mem": n((N, U)).astype(np.float32),
        "offs": striped(np.random.permutation(T)[:S]),
        "n1": striped8(np.stack([np.random.permutation(H) for _ in range(8)])),
        "n2": striped8(np.stack([np.random.permutation(H) for _ in range(8)])),
        "n3": striped8(np.stack([np.random.permutation(U)[:H] for _ in range(8)])),
    }


def reference(x_words, x_scales, wa, gt, w1_words, w1_scales, mem, offs, n1, n2, n3):
    xq = unpack_weight(x_words, x_scales)[:, unstriped(offs)]
    y = xq.T @ mxq(f64(wa), 0, "e4m3")
    st = y - (y[np.arange(S)[:, None], runs(n1, S)])
    z = f64(gt) * (st / (np.abs(st[np.arange(S)[:, None], runs(n2, S)]) + 0.5))
    h = unpack_weight(w1_words, w1_scales).T @ mxq(z, 0, "e4m3")
    nw = np.maximum(h, 0.5 * (f64(mem)[np.arange(N)[:, None], runs(n3, N)]))
    out = f64(mem).copy()
    out[np.arange(N)[:, None], runs(n3, N)] = nw
    return (out,) + planes(out)

@@ -1,0 +1,223 @@
+from contextlib import ExitStack
+
+import concourse.mybir as mybir
+
+K, T, S, N, H, U = 512, 2048, 512, 512, 512, 1024
+FLOPS = 2 * S * K * H + 2 * N * S * H
+
+F32 = mybir.dt.float32
+BF16 = mybir.dt.bfloat16
+I32 = mybir.dt.int32
+U32 = mybir.dt.uint32
+U16 = mybir.dt.uint16
+U8 = mybir.dt.uint8
+FP8X4 = mybir.dt.float8_e4m3fn_x4
+ACT = mybir.ActivationFunctionType
+ALU = mybir.AluOpType
+
+P = 128
+PACK = 4
+CHUNKS = (128, 128, 128, 128)
+G1V = 2
+G2V = 2
+WARM = 0
+WAV = 256
+NA = 2
+YCV = 1
+OLDV = 2
+GM = 9
+GC = 0
+OCH = 256
+NOCH = U // OCH
+
+
+def tile_picked_tokhopnpagex_none_po_kernel(
+    tc, x_words, x_scales, wa, gt, w1_words, w1_scales, mem, offs, n1, n2, n3, out_0, out_1, out_2
+):
+    nc = tc.nc
+    with ExitStack() as ctx:
+        keep = ctx.enter_context(tc.tile_pool(name="keep", bufs=1))
+        psum = ctx.enter_context(tc.psum_pool(name="psum", bufs=1))
+
+        def sb(shape, dtype, name):
+            return keep.tile(shape, dtype, name=name, align_bytes=64)
+
+        def cols(lst, c0, c1):
+            return lst[:, c0 // 16 : c1 // 16]
+
+        offs_t = keep.tile([P, S // 16], U16, name="offs_t")
+        n1_t = keep.tile([P, H // 16], U16, name="n1_t")
+        n2_t = keep.tile([P, H // 16], U16, name="n2_t")
+        n3_t = keep.tile([P, H // 16], U16, name="n3_t")
+        wa_raw = sb([P, PACK, H], F32, "wa_raw")
+        xw = sb([P, T], U32, "xw")
+        xs = sb([P, T], U8, "xs")
+        w1w = sb([P, N], U32, "w1w")
+        w1s = sb([P, N], U8, "w1s")
+        gt_t = sb([P, PACK], F32, "gt_t")
+        page = [sb([P, U], F32, "page%d" % t) for t in range(PACK)]
+
+        nc.gpsimd.memset(xs[:].bitcast(I32), 0)
+        nc.gpsimd.memset(w1s[:].bitcast(I32), 0)
+        if WARM:
+            warm = sb([P, 1], F32, "warm")
+            nc.gpsimd.memset(warm[:], 1.0)
+            nc.scalar.activation(warm[:], warm[:], ACT.Abs_reciprocal_sqrt)
+        nc.sync.dma_start(out=wa_raw[:], in_=wa.rearrange("(p j) w -> p j w", j=PACK))
+        for q in range(4):
+            nc.sync.dma_start(out=xs[32 * q : 32 * q + 4, :].bitcast(I32), in_=x_scales[0, 4 * q : 4 * q + 4, :].bitcast(I32))
+        nc.sync.dma_start(offs_t[:], offs)
+        nc.sync.dma_start(out=xw[:].bitcast(I32), in_=x_words[0].rearrange("p n t -> p (n t)").bitcast(I32))
+        nc.sync.dma_start(n1_t[:], n1)
+        nc.sync.dma_start(out=w1w[:].bitcast(I32), in_=w1_words[0].rearrange("p n t -> p (n t)").bitcast(I32))
+        for q in range(4):
+            nc.sync.dma_start(out=w1s[32 * q : 32 * q + 4, :].bitcast(I32), in_=w1_scales[0, 4 * q : 4 * q + 4, :].bitcast(I32))
+        nc.sync.dma_start(out=gt_t[:], in_=gt.rearrange("(p t) o -> p (t o)", t=PACK))
+        nc.sync.dma_start(n2_t[:], n2)
+        nc.sync.dma_start(n3_t[:], n3)
+        mem_v = mem.rearrange("(p t) u -> p t u", t=PACK)
+        out_v = out_0.rearrange("(p t) u -> p t u", t=PACK)
+        for t in range(PACK):
+            nc.sync.dma_start(out=page[t][:], in_=mem_v[:, t, :])
+
+        parts = ((0, H - WAV), (H - WAV, H))
+        wa_bf = [sb([P, b - a, PACK], BF16, "wa_bf%d" % a) for a, b in parts]
+        wa_q = sb([P, H], U32, "wa_q")
+        wa_s = sb([P, H], U8, "wa_s")
+        xsg = sb([P, PACK, P], U8, "xsg")
+        xwg = sb([P, PACK, P], U32, "xwg")
+        nc.vector.tensor_copy(xsg[:].rearrange("p t m -> p m t"), xs[:].indirect(offs_t[:]))
+        for h, (a, b) in enumerate(parts):
+            dst = wa_bf[h][:].rearrange("p (c i) t -> p c t i", i=4)
+            src = wa_raw[:, :, a:b].rearrange("p t (c i) -> p c t i", i=4)
+            if h == 1:
+                nc.vector.tensor_copy(out=dst, in_=src)
+            else:
+                nc.scalar.activation(dst, src, ACT.Copy)
+        for h, (a, b) in enumerate(parts):
+            nc.vector.quantize_mx(out=wa_q[:, a:b].bitcast(FP8X4), scales=wa_s[:, a:b], in_=wa_bf[h][:].rearrange("p c t -> p (c t)"))
+
+        nc.vector.tensor_copy(xwg[:].rearrange("p t m -> p m t"), xw[:].indirect(offs_t[:]))
+
+        w1wd = sb([P, PACK, P], U32, "w1wd")
+        w1sd = sb([P, PACK, P], U8, "w1sd")
+        nc.gpsimd.tensor_copy(out=w1wd[:], in_=w1w[:].rearrange("p (m t) -> p t m", t=PACK))
+        nc.gpsimd.tensor_copy(out=w1sd[:], in_=w1s[:].rearrange("p (m t) -> p t m", t=PACK))
+
+        y_ps = [psum.tile([P, H], F32, name="y_ps%d" % t, tag="bank%d" % t) for t in range(PACK)]
+        for t in range(PACK):
+            nc.tensor.matmul_mx(out=y_ps[t][:], lhsT=xwg[:, t, :].bitcast(FP8X4), lhsT_scale=xsg[:, t, :],
+                                rhs=wa_q[:].bitcast(FP8X4), rhs_scale=wa_s[:], start=True, stop=True)
+
+        y_sb = [sb([P, H], F32, "y_sb%d" % t) for t in range(PACK)]
+        y_n1 = [sb([P, H], F32, "y_n1_%d" % t) for t in range(PACK)]
+        st = [sb([P, H], F32, "st%d" % t) for t in range(PACK)]
+        stg = sb([P, PACK, H], F32, "stg")
+
+        def gather(on_vector, out, window, offsets):
+            if on_vector:
+                nc.vector.tensor_copy(out, window.indirect(offsets))
+            else:
+                nc.scalar.activation(out, window.indirect(offsets), ACT.Copy)
+
+        def fetch_n1(t, h):
+            c0 = h * (H // 2)
+            gather(t < G1V, y_n1[t][:, c0 : c0 + H // 2], y_sb[t][:], cols(n1_t, c0, c0 + H // 2))
+
+        def subtract(t):
+            nc.vector.tensor_tensor(st[t][:], y_ps[t][:], y_n1[t][:], ALU.subtract)
+            nc.gpsimd.tensor_scalar(stg[:, t, :], st[t][:], gt_t[:, t : t + 1], 1.0, ALU.mult, ALU.mult)
+
+        for t in range(PACK):
+            (nc.vector.tensor_copy if t < YCV else nc.scalar.copy)(y_sb[t][:], y_ps[t][:])
+        for t in range(PACK):
+            fetch_n1(t, 0)
+            if t > 0:
+                subtract(t - 1)
+            fetch_n1(t, 1)
+        subtract(PACK - 1)
+
+        old = sb([P, NA, H], F32, "old")
+        new_a = sb([P, NA, H], F32, "new_a")
+        new_b = {t: sb([P, H], F32, "new_b%d" % t) for t in range(NA, PACK)}
+        h_late = {t: psum.tile([P, H], F32, name="h_late%d" % t, tag="bank%d" % (t - NA)) for t in range(NA, PACK)}
+
+        def inverse(den, a, b, square=True):
+            v = den[:, a:b, :]
+            nc.scalar.activation(v, v, ACT.Abs)
+            nc.scalar.activation(v, v, ACT.Abs_reciprocal_sqrt, bias=0.5)
+            if square:
+                nc.scalar.activation(v, v, ACT.Square)
+
+        c0 = 0
+        for c, ch in enumerate(CHUNKS):
+            c1 = c0 + ch
+            cc = slice(c0, c1)
+            den = keep.tile([P, PACK, ch], F32, name="den%d" % c, tag="den%d" % c, align_bytes=64)
+            for t in range(PACK):
+                gather(c == 0 and t >= PACK - G2V, den[:, t, :], st[t][:], cols(n2_t, c0, c1))
+                if c == 0 and t == 1:
+                    inverse(den, 0, 2)
+            if c == 0:
+                inverse(den, 2, 4)
+                for t in range(NA):
+                    gather(t < OLDV, old[:, t, :], page[t][:], n3_t[:])
+            else:
+                inverse(den, 0, 4, c < GM)
+            z_bf = sb([P, ch, PACK], BF16, "z_bf%d" % c)
+            if c >= GM:
+                nc.gpsimd.tensor_tensor(stg[:, :, cc], stg[:, :, cc], den[:], ALU.mult)
+            (nc.gpsimd if c >= GM else nc.vector).tensor_tensor(
+                z_bf[:].rearrange("p (c i) t -> p c t i", i=4),
+                stg[:, :, cc].rearrange("p t (c i) -> p c t i", i=4),
+                den[:].rearrange("p t (c i) -> p c t i", i=4),
+                ALU.mult,
+            )
+            z_q = sb([P, ch], U32, "z_q%d" % c)
+            z_s = sb([P, ch], U8, "z_s%d" % c)
+            nc.vector.quantize_mx(out=z_q[:].bitcast(FP8X4), scales=z_s[:], in_=z_bf[:].rearrange("p c t -> p (c t)"))
+            h_ps = psum.tile([P, NA, ch], F32, name="h_ps%d" % c, tag="bank%d" % (4 + c))
+            for t in range(PACK):
+                dst = h_ps[:, t, :] if t < NA else h_late[t][:, cc]
+                nc.tensor.matmul_mx(out=dst, lhsT=w1wd[:, t, :].bitcast(FP8X4), lhsT_scale=w1sd[:, t, :],
+                                    rhs=z_q[:].bitcast(FP8X4), rhs_scale=z_s[:], start=True, stop=True)
+            nc.vector.scalar_tensor_tensor(new_a[:, :, cc], old[:, :, cc], 0.5, h_ps[:], ALU.mult, ALU.max)
+            for t in range(NA):
+                nc.vector.tensor_copy(page[t][:].indirect(cols(n3_t, c0, c1)), new_a[:, t, cc])
+            c0 = c1
+
+        planes = sb([P, 2, U], BF16, "planes")
+        o_bf = [sb([P, OCH, PACK], BF16, "o_bf%d" % k) for k in range(NOCH)]
+        o_s = sb([P, U], U8, "o_s")
+        words_v = out_1[0].rearrange("p n t -> p (n t)").bitcast(I32)
+
+        for t in range(NA, PACK):
+            old_t = keep.tile([P, H], F32, name="old%d" % t, tag="den%d" % min(len(CHUNKS) - 1, t - NA + 2), align_bytes=64)
+            gather(False, old_t[:], page[t][:], n3_t[:])
+            nc.vector.scalar_tensor_tensor(new_b[t][:], old_t[:], 0.5, h_late[t][:], ALU.mult, ALU.max)
+        for t in range(PACK):
+            if t >= NA:
+                nc.vector.tensor_copy(page[t][:].indirect(n3_t[:]), new_b[t][:])
+            nc.sync.dma_start(out=out_v[:, t, :], in_=page[t][:])
+            if t < 2:
+                for h in range(2):
+                    hc = slice(h * (U // 2), (h + 1) * (U // 2))
+                    if GC:
+                        nc.gpsimd.tensor_scalar(planes[:, t, hc], page[t][:, hc], 1.0, 1.0, ALU.mult, ALU.mult)
+                    else:
+                        nc.scalar.copy(planes[:, t, hc], page[t][:, hc])
+            if t == 1:
+                for k in range(NOCH):
+                    kc = slice(k * OCH, (k + 1) * OCH)
+                    nc.scalar.copy(out=o_bf[k][:, :, 0:2], in_=planes[:, :, kc].rearrange("p t c -> p c t"))
+        for t in (2, 3):
+            for k in range(NOCH):
+                copy = nc.scalar.copy if k < 2 else nc.vector.tensor_copy
+                copy(o_bf[k][:, :, t], page[t][:, k * OCH : (k + 1) * OCH])
+        for k in (2, 3, 0, 1):
+            kc = slice(k * OCH, (k + 1) * OCH)
+            o_q = sb([P, OCH], U32, "o_q%d" % k)
+            nc.vector.quantize_mx(out=o_q[:].bitcast(FP8X4), scales=o_s[:, kc], in_=o_bf[k][:].rearrange("p c t -> p (c t)"))
+            nc.sync.dma_start(out=words_v[:, kc], in_=o_q[:].bitcast(I32))
+        for q in range(4):
+            nc.scalar.dma_start(out=out_2[0, 4 * q : 4 * q + 4, :].bitcast(I32), in_=o_s[32 * q : 32 * q + 4, :].bitcast(I32))

@@ -20,7 +20,7 @@ PACK = 4
 CHUNKS = (128, 128, 128, 128)
 G1V = 2
 G2V = 2
-WARM = 0
+WARM = 1
 WAV = 256
 NA = 2
 YCV = 1

@@ -17,18 +17,14 @@ ALU = mybir.AluOpType
 
 P = 128
 PACK = 4
-CHUNKS = (128, 128, 128, 128)
-G1V = 2
-G2V = 2
-WARM = 1
-WAV = 256
-NA = 2
-YCV = 1
-OLDV = 2
-GM = 9
-GC = 0
-OCH = 256
-NOCH = U // OCH
+QUADS = 4
+HALF = H // 2
+CHUNK = 128
+CHUNKS = H // CHUNK
+OUT_CHUNK = 256
+OUT_CHUNKS = U // OUT_CHUNK
+N1_ON_VECTOR = 2
+N2_ON_SCALAR = 6
 
 
 def tile_picked_tokhopnpagex_none_po_kernel(
@@ -39,11 +35,32 @@ def tile_picked_tokhopnpagex_none_po_kernel(
         keep = ctx.enter_context(tc.tile_pool(name="keep", bufs=1))
         psum = ctx.enter_context(tc.psum_pool(name="psum", bufs=1))
 
-        def sb(shape, dtype, name):
-            return keep.tile(shape, dtype, name=name, align_bytes=64)
+        def sb(shape, dtype, name, reuse=None):
+            return keep.tile(shape, dtype, name=name, tag=reuse or name, align_bytes=64)
 
-        def cols(lst, c0, c1):
-            return lst[:, c0 // 16 : c1 // 16]
+        def entries(list_tile, j0, j1):
+            return list_tile[:, j0 // 16 : j1 // 16]
+
+        def gather(on_vector, out, window, offsets):
+            if on_vector:
+                nc.vector.tensor_copy(out, window.indirect(offsets))
+            else:
+                nc.scalar.activation(out, window.indirect(offsets), ACT.Copy)
+
+        def interleaved(ap):
+            return ap.rearrange("p (c i) t -> p c t i", i=2)
+
+        def by_tile(ap):
+            return ap.rearrange("p t (c i) -> p c t i", i=2)
+
+        def as_words(dram_bytes):
+            return dram_bytes[0].rearrange("p n t -> p (n t)").bitcast(I32)
+
+        def load_scale_rows(plane, dram_scales):
+            for q in range(QUADS):
+                nc.sync.dma_start(
+                    out=plane[32 * q : 32 * q + 4, :].bitcast(I32), in_=dram_scales[0, 4 * q : 4 * q + 4, :].bitcast(I32)
+                )
 
         offs_t = keep.tile([P, S // 16], U16, name="offs_t")
         n1_t = keep.tile([P, H // 16], U16, name="n1_t")
@@ -59,165 +76,174 @@ def tile_picked_tokhopnpagex_none_po_kernel(
 
         nc.gpsimd.memset(xs[:].bitcast(I32), 0)
         nc.gpsimd.memset(w1s[:].bitcast(I32), 0)
-        if WARM:
-            warm = sb([P, 1], F32, "warm")
-            nc.gpsimd.memset(warm[:], 1.0)
-            nc.scalar.activation(warm[:], warm[:], ACT.Abs_reciprocal_sqrt)
+        warm = sb([P, 1], F32, "warm")
+        nc.gpsimd.memset(warm[:], 1.0)
+        nc.scalar.activation(warm[:], warm[:], ACT.Abs_reciprocal_sqrt)
+
         nc.sync.dma_start(out=wa_raw[:], in_=wa.rearrange("(p j) w -> p j w", j=PACK))
-        for q in range(4):
-            nc.sync.dma_start(out=xs[32 * q : 32 * q + 4, :].bitcast(I32), in_=x_scales[0, 4 * q : 4 * q + 4, :].bitcast(I32))
+        load_scale_rows(xs, x_scales)
         nc.sync.dma_start(offs_t[:], offs)
-        nc.sync.dma_start(out=xw[:].bitcast(I32), in_=x_words[0].rearrange("p n t -> p (n t)").bitcast(I32))
+        nc.sync.dma_start(out=xw[:].bitcast(I32), in_=as_words(x_words))
         nc.sync.dma_start(n1_t[:], n1)
-        nc.sync.dma_start(out=w1w[:].bitcast(I32), in_=w1_words[0].rearrange("p n t -> p (n t)").bitcast(I32))
-        for q in range(4):
-            nc.sync.dma_start(out=w1s[32 * q : 32 * q + 4, :].bitcast(I32), in_=w1_scales[0, 4 * q : 4 * q + 4, :].bitcast(I32))
+        nc.sync.dma_start(out=w1w[:].bitcast(I32), in_=as_words(w1_words))
+        load_scale_rows(w1s, w1_scales)
         nc.sync.dma_start(out=gt_t[:], in_=gt.rearrange("(p t) o -> p (t o)", t=PACK))
         nc.sync.dma_start(n2_t[:], n2)
         nc.sync.dma_start(n3_t[:], n3)
-        mem_v = mem.rearrange("(p t) u -> p t u", t=PACK)
-        out_v = out_0.rearrange("(p t) u -> p t u", t=PACK)
+        mem_rows = mem.rearrange("(p t) u -> p t u", t=PACK)
+        out_rows = out_0.rearrange("(p t) u -> p t u", t=PACK)
         for t in range(PACK):
-            nc.sync.dma_start(out=page[t][:], in_=mem_v[:, t, :])
+            nc.sync.dma_start(out=page[t][:], in_=mem_rows[:, t, :])
 
-        parts = ((0, H - WAV), (H - WAV, H))
-        wa_bf = [sb([P, b - a, PACK], BF16, "wa_bf%d" % a) for a, b in parts]
+        halves = (slice(0, HALF), slice(HALF, H))
+        wa_bf = [sb([P, HALF, PACK], BF16, "wa_bf%d" % h) for h in range(2)]
         wa_q = sb([P, H], U32, "wa_q")
         wa_s = sb([P, H], U8, "wa_s")
-        xsg = sb([P, PACK, P], U8, "xsg")
-        xwg = sb([P, PACK, P], U32, "xwg")
-        nc.vector.tensor_copy(xsg[:].rearrange("p t m -> p m t"), xs[:].indirect(offs_t[:]))
-        for h, (a, b) in enumerate(parts):
-            dst = wa_bf[h][:].rearrange("p (c i) t -> p c t i", i=4)
-            src = wa_raw[:, :, a:b].rearrange("p t (c i) -> p c t i", i=4)
-            if h == 1:
-                nc.vector.tensor_copy(out=dst, in_=src)
-            else:
-                nc.scalar.activation(dst, src, ACT.Copy)
-        for h, (a, b) in enumerate(parts):
-            nc.vector.quantize_mx(out=wa_q[:, a:b].bitcast(FP8X4), scales=wa_s[:, a:b], in_=wa_bf[h][:].rearrange("p c t -> p (c t)"))
+        xs_picked = sb([P, PACK, P], U8, "xs_picked")
+        xw_picked = sb([P, PACK, P], U32, "xw_picked")
+        nc.vector.tensor_copy(xs_picked[:].rearrange("p t m -> p m t"), xs[:].indirect(offs_t[:]))
+        nc.scalar.activation(interleaved(wa_bf[0][:]), by_tile(wa_raw[:, :, halves[0]]), ACT.Copy)
+        nc.vector.tensor_copy(out=interleaved(wa_bf[1][:]), in_=by_tile(wa_raw[:, :, halves[1]]))
+        for h in range(2):
+            nc.vector.quantize_mx(
+                out=wa_q[:, halves[h]].bitcast(FP8X4),
+                scales=wa_s[:, halves[h]],
+                in_=wa_bf[h][:].rearrange("p c t -> p (c t)"),
+            )
+        nc.vector.tensor_copy(xw_picked[:].rearrange("p t m -> p m t"), xw[:].indirect(offs_t[:]))
 
-        nc.vector.tensor_copy(xwg[:].rearrange("p t m -> p m t"), xw[:].indirect(offs_t[:]))
-
-        w1wd = sb([P, PACK, P], U32, "w1wd")
-        w1sd = sb([P, PACK, P], U8, "w1sd")
-        nc.gpsimd.tensor_copy(out=w1wd[:], in_=w1w[:].rearrange("p (m t) -> p t m", t=PACK))
-        nc.gpsimd.tensor_copy(out=w1sd[:], in_=w1s[:].rearrange("p (m t) -> p t m", t=PACK))
+        w1w_dealt = sb([P, PACK, P], U32, "w1w_dealt")
+        w1s_dealt = sb([P, PACK, P], U8, "w1s_dealt")
+        nc.gpsimd.tensor_copy(out=w1w_dealt[:], in_=w1w[:].rearrange("p (m t) -> p t m", t=PACK))
+        nc.gpsimd.tensor_copy(out=w1s_dealt[:], in_=w1s[:].rearrange("p (m t) -> p t m", t=PACK))
 
         y_ps = [psum.tile([P, H], F32, name="y_ps%d" % t, tag="bank%d" % t) for t in range(PACK)]
         for t in range(PACK):
-            nc.tensor.matmul_mx(out=y_ps[t][:], lhsT=xwg[:, t, :].bitcast(FP8X4), lhsT_scale=xsg[:, t, :],
-                                rhs=wa_q[:].bitcast(FP8X4), rhs_scale=wa_s[:], start=True, stop=True)
+            nc.tensor.matmul_mx(
+                out=y_ps[t][:],
+                lhsT=xw_picked[:, t, :].bitcast(FP8X4),
+                lhsT_scale=xs_picked[:, t, :],
+                rhs=wa_q[:].bitcast(FP8X4),
+                rhs_scale=wa_s[:],
+                start=True,
+                stop=True,
+            )
 
         y_sb = [sb([P, H], F32, "y_sb%d" % t) for t in range(PACK)]
         y_n1 = [sb([P, H], F32, "y_n1_%d" % t) for t in range(PACK)]
         st = [sb([P, H], F32, "st%d" % t) for t in range(PACK)]
-        stg = sb([P, PACK, H], F32, "stg")
-
-        def gather(on_vector, out, window, offsets):
-            if on_vector:
-                nc.vector.tensor_copy(out, window.indirect(offsets))
-            else:
-                nc.scalar.activation(out, window.indirect(offsets), ACT.Copy)
+        st_gt = sb([P, PACK, H], F32, "st_gt")
 
         def fetch_n1(t, h):
-            c0 = h * (H // 2)
-            gather(t < G1V, y_n1[t][:, c0 : c0 + H // 2], y_sb[t][:], cols(n1_t, c0, c0 + H // 2))
+            cols = halves[h]
+            gather(t < N1_ON_VECTOR, y_n1[t][:, cols], y_sb[t][:], entries(n1_t, cols.start, cols.stop))
 
         def subtract(t):
             nc.vector.tensor_tensor(st[t][:], y_ps[t][:], y_n1[t][:], ALU.subtract)
-            nc.gpsimd.tensor_scalar(stg[:, t, :], st[t][:], gt_t[:, t : t + 1], 1.0, ALU.mult, ALU.mult)
+            nc.gpsimd.tensor_scalar(st_gt[:, t, :], st[t][:], gt_t[:, t : t + 1], 1.0, ALU.mult, ALU.mult)
 
-        for t in range(PACK):
-            (nc.vector.tensor_copy if t < YCV else nc.scalar.copy)(y_sb[t][:], y_ps[t][:])
+        nc.vector.tensor_copy(y_sb[0][:], y_ps[0][:])
+        for t in range(1, PACK):
+            nc.scalar.copy(y_sb[t][:], y_ps[t][:])
         for t in range(PACK):
             fetch_n1(t, 0)
             if t > 0:
                 subtract(t - 1)
             fetch_n1(t, 1)
+        old = [sb([P, H], F32, "old0", reuse="y_sb3"), sb([P, H], F32, "old1", reuse="y_n1_3")]
+        gather(False, old[0][:], page[0][:], n3_t[:])
         subtract(PACK - 1)
 
-        old = sb([P, NA, H], F32, "old")
-        new_a = sb([P, NA, H], F32, "new_a")
-        new_b = {t: sb([P, H], F32, "new_b%d" % t) for t in range(NA, PACK)}
-        h_late = {t: psum.tile([P, H], F32, name="h_late%d" % t, tag="bank%d" % (t - NA)) for t in range(NA, PACK)}
+        new_late = {t: sb([P, H], F32, "new_late%d" % t) for t in (2, 3)}
+        h_late = {t: psum.tile([P, H], F32, name="h_late%d" % t, tag="bank%d" % (t - 2)) for t in (2, 3)}
 
-        def inverse(den, a, b, square=True):
-            v = den[:, a:b, :]
-            nc.scalar.activation(v, v, ACT.Abs)
-            nc.scalar.activation(v, v, ACT.Abs_reciprocal_sqrt, bias=0.5)
-            if square:
+        def invert(den):
+            parts = (den[:, 0:2, :], den[:, 2:4, :])
+            for v in parts:
+                nc.scalar.activation(v, v, ACT.Abs)
+            for v in parts:
+                nc.scalar.activation(v, v, ACT.Abs_reciprocal_sqrt, bias=0.5)
+            for v in parts:
                 nc.scalar.activation(v, v, ACT.Square)
 
-        c0 = 0
-        for c, ch in enumerate(CHUNKS):
-            c1 = c0 + ch
-            cc = slice(c0, c1)
-            den = keep.tile([P, PACK, ch], F32, name="den%d" % c, tag="den%d" % c, align_bytes=64)
+        def write_chunk(c, t, h_ps, reuse):
+            cols = slice(c * CHUNK, (c + 1) * CHUNK)
+            new = sb([P, CHUNK], F32, "new%d_%d" % (c, t), reuse=reuse)
+            nc.vector.scalar_tensor_tensor(new[:], old[t][:, cols], 0.5, h_ps[:, t, :], ALU.mult, ALU.max)
+            nc.vector.tensor_copy(page[t][:].indirect(entries(n3_t, cols.start, cols.stop)), new[:])
+
+        den_buffer = ("den0", "y_n1_2", "y_n1_1", "den0")
+        h_early = []
+        for c in range(CHUNKS):
+            cols = slice(c * CHUNK, (c + 1) * CHUNK)
+            den = sb([P, PACK, CHUNK], F32, "den%d" % c, reuse=den_buffer[c])
             for t in range(PACK):
-                gather(c == 0 and t >= PACK - G2V, den[:, t, :], st[t][:], cols(n2_t, c0, c1))
-                if c == 0 and t == 1:
-                    inverse(den, 0, 2)
-            if c == 0:
-                inverse(den, 2, 4)
-                for t in range(NA):
-                    gather(t < OLDV, old[:, t, :], page[t][:], n3_t[:])
-            else:
-                inverse(den, 0, 4, c < GM)
-            z_bf = sb([P, ch, PACK], BF16, "z_bf%d" % c)
-            if c >= GM:
-                nc.gpsimd.tensor_tensor(stg[:, :, cc], stg[:, :, cc], den[:], ALU.mult)
-            (nc.gpsimd if c >= GM else nc.vector).tensor_tensor(
-                z_bf[:].rearrange("p (c i) t -> p c t i", i=4),
-                stg[:, :, cc].rearrange("p t (c i) -> p c t i", i=4),
-                den[:].rearrange("p t (c i) -> p c t i", i=4),
-                ALU.mult,
-            )
-            z_q = sb([P, ch], U32, "z_q%d" % c)
-            z_s = sb([P, ch], U8, "z_s%d" % c)
+                on_vector = PACK * (CHUNKS - 1 - c) + t >= N2_ON_SCALAR
+                gather(on_vector, den[:, t, :], st[t][:], entries(n2_t, cols.start, cols.stop))
+            invert(den)
+            if c == 1:
+                gather(True, old[1][:], page[1][:], n3_t[:])
+            z_bf = sb([P, CHUNK, PACK], BF16, "z_bf%d" % c)
+            nc.vector.tensor_tensor(interleaved(z_bf[:]), by_tile(st_gt[:, :, cols]), by_tile(den[:]), ALU.mult)
+            z_q = sb([P, CHUNK], U32, "z_q%d" % c)
+            z_s = sb([P, CHUNK], U8, "z_s%d" % c)
             nc.vector.quantize_mx(out=z_q[:].bitcast(FP8X4), scales=z_s[:], in_=z_bf[:].rearrange("p c t -> p (c t)"))
-            h_ps = psum.tile([P, NA, ch], F32, name="h_ps%d" % c, tag="bank%d" % (4 + c))
+            h_ps = psum.tile([P, 2, CHUNK], F32, name="h_ps%d" % c, tag="bank%d" % (PACK + c))
+            h_early.append(h_ps)
             for t in range(PACK):
-                dst = h_ps[:, t, :] if t < NA else h_late[t][:, cc]
-                nc.tensor.matmul_mx(out=dst, lhsT=w1wd[:, t, :].bitcast(FP8X4), lhsT_scale=w1sd[:, t, :],
-                                    rhs=z_q[:].bitcast(FP8X4), rhs_scale=z_s[:], start=True, stop=True)
-            nc.vector.scalar_tensor_tensor(new_a[:, :, cc], old[:, :, cc], 0.5, h_ps[:], ALU.mult, ALU.max)
-            for t in range(NA):
-                nc.vector.tensor_copy(page[t][:].indirect(cols(n3_t, c0, c1)), new_a[:, t, cc])
-            c0 = c1
+                nc.tensor.matmul_mx(
+                    out=h_ps[:, t, :] if t < 2 else h_late[t][:, cols],
+                    lhsT=w1w_dealt[:, t, :].bitcast(FP8X4),
+                    lhsT_scale=w1s_dealt[:, t, :],
+                    rhs=z_q[:].bitcast(FP8X4),
+                    rhs_scale=z_s[:],
+                    start=True,
+                    stop=True,
+                )
+            if c > 0:
+                write_chunk(c - 1, 1, h_early[c - 1], den_buffer[c])
+            write_chunk(c, 0, h_ps, None)
+        write_chunk(CHUNKS - 1, 1, h_early[CHUNKS - 1], None)
 
-        planes = sb([P, 2, U], BF16, "planes")
-        o_bf = [sb([P, OCH, PACK], BF16, "o_bf%d" % k) for k in range(NOCH)]
+        early_bf = sb([P, 2, U], BF16, "early_bf")
+        o_bf = [sb([P, OUT_CHUNK, PACK], BF16, "o_bf%d" % k) for k in range(OUT_CHUNKS)]
         o_s = sb([P, U], U8, "o_s")
-        words_v = out_1[0].rearrange("p n t -> p (n t)").bitcast(I32)
 
-        for t in range(NA, PACK):
-            old_t = keep.tile([P, H], F32, name="old%d" % t, tag="den%d" % min(len(CHUNKS) - 1, t - NA + 2), align_bytes=64)
-            gather(False, old_t[:], page[t][:], n3_t[:])
-            nc.vector.scalar_tensor_tensor(new_b[t][:], old_t[:], 0.5, h_late[t][:], ALU.mult, ALU.max)
-        for t in range(PACK):
-            if t >= NA:
-                nc.vector.tensor_copy(page[t][:].indirect(n3_t[:]), new_b[t][:])
-            nc.sync.dma_start(out=out_v[:, t, :], in_=page[t][:])
-            if t < 2:
-                for h in range(2):
-                    hc = slice(h * (U // 2), (h + 1) * (U // 2))
-                    if GC:
-                        nc.gpsimd.tensor_scalar(planes[:, t, hc], page[t][:, hc], 1.0, 1.0, ALU.mult, ALU.mult)
-                    else:
-                        nc.scalar.copy(planes[:, t, hc], page[t][:, hc])
-            if t == 1:
-                for k in range(NOCH):
-                    kc = slice(k * OCH, (k + 1) * OCH)
-                    nc.scalar.copy(out=o_bf[k][:, :, 0:2], in_=planes[:, :, kc].rearrange("p t c -> p c t"))
+        def out_cols(k):
+            return slice(k * OUT_CHUNK, (k + 1) * OUT_CHUNK)
+
         for t in (2, 3):
-            for k in range(NOCH):
-                copy = nc.scalar.copy if k < 2 else nc.vector.tensor_copy
-                copy(o_bf[k][:, :, t], page[t][:, k * OCH : (k + 1) * OCH])
+            old_t = sb([P, H], F32, "old%d" % t, reuse="z_bf%d" % t)
+            gather(False, old_t[:], page[t][:], n3_t[:])
+            nc.vector.scalar_tensor_tensor(new_late[t][:], old_t[:], 0.5, h_late[t][:], ALU.mult, ALU.max)
+
+        for t in (0, 1):
+            nc.sync.dma_start(out=out_rows[:, t, :], in_=page[t][:])
+            for h in range(2):
+                cols = slice(h * (U // 2), (h + 1) * (U // 2))
+                nc.scalar.copy(early_bf[:, t, cols], page[t][:, cols])
+        for k in range(OUT_CHUNKS):
+            nc.scalar.copy(out=o_bf[k][:, :, 0:2], in_=early_bf[:, :, out_cols(k)].rearrange("p t c -> p c t"))
+        for t in (2, 3):
+            nc.vector.tensor_copy(page[t][:].indirect(n3_t[:]), new_late[t][:])
+            nc.sync.dma_start(out=out_rows[:, t, :], in_=page[t][:])
+        late_bf = sb([P, 2, U // 2], BF16, "late_bf")
+        nc.scalar.copy(late_bf[:, 0, :], page[2][:, U // 2 :])
+        for t in (2, 3):
+            for k in range(2):
+                nc.scalar.copy(o_bf[k][:, :, t], page[t][:, out_cols(k)])
+        for k in range(2):
+            nc.vector.tensor_copy(late_bf[:, 1, out_cols(k)], page[3][:, out_cols(2 + k)])
+        for k in range(2):
+            nc.vector.tensor_copy(out=o_bf[2 + k][:, :, 2:4], in_=late_bf[:, :, out_cols(k)].rearrange("p t c -> p c t"))
+
         for k in (2, 3, 0, 1):
-            kc = slice(k * OCH, (k + 1) * OCH)
-            o_q = sb([P, OCH], U32, "o_q%d" % k)
-            nc.vector.quantize_mx(out=o_q[:].bitcast(FP8X4), scales=o_s[:, kc], in_=o_bf[k][:].rearrange("p c t -> p (c t)"))
-            nc.sync.dma_start(out=words_v[:, kc], in_=o_q[:].bitcast(I32))
-        for q in range(4):
-            nc.scalar.dma_start(out=out_2[0, 4 * q : 4 * q + 4, :].bitcast(I32), in_=o_s[32 * q : 32 * q + 4, :].bitcast(I32))
+            o_q = sb([P, OUT_CHUNK], U32, "o_q%d" % k)
+            nc.vector.quantize_mx(
+                out=o_q[:].bitcast(FP8X4), scales=o_s[:, out_cols(k)], in_=o_bf[k][:].rearrange("p c t -> p (c t)")
+            )
+            nc.sync.dma_start(out=as_words(out_1)[:, out_cols(k)], in_=o_q[:].bitcast(I32))
+        for q in range(QUADS):
+            nc.scalar.dma_start(
+                out=out_2[0, 4 * q : 4 * q + 4, :].bitcast(I32), in_=o_s[32 * q : 32 * q + 4, :].bitcast(I32)
+            )

@@ -150,15 +150,13 @@ def tile_picked_tokhopnpagex_none_po_kernel(
             if t > 0:
                 subtract(t - 1)
             fetch_n1(t, 1)
-        old = [sb([P, H], F32, "old0", reuse="y_sb3"), sb([P, H], F32, "old1", reuse="y_n1_3")]
-        gather(False, old[0][:], page[0][:], n3_t[:])
         subtract(PACK - 1)
+        old = {1: sb([P, H], F32, "old1", reuse="y_n1_3")}
 
         new_late = {t: sb([P, H], F32, "new_late%d" % t) for t in (2, 3)}
         h_late = {t: psum.tile([P, H], F32, name="h_late%d" % t, tag="bank%d" % (t - 2)) for t in (2, 3)}
 
-        def invert(den):
-            parts = (den[:, 0:2, :], den[:, 2:4, :])
+        def invert(*parts):
             for v in parts:
                 nc.scalar.activation(v, v, ACT.Abs)
             for v in parts:
@@ -172,7 +170,7 @@ def tile_picked_tokhopnpagex_none_po_kernel(
             nc.vector.scalar_tensor_tensor(new[:], old[t][:, cols], 0.5, h_ps[:, t, :], ALU.mult, ALU.max)
             nc.vector.tensor_copy(page[t][:].indirect(entries(n3_t, cols.start, cols.stop)), new[:])
 
-        den_buffer = ("den0", "y_n1_2", "y_n1_1", "den0")
+        den_buffer = ("den0", "y_n1_2", "y_n1_1", "z_bf0")
         h_early = []
         for c in range(CHUNKS):
             cols = slice(c * CHUNK, (c + 1) * CHUNK)
@@ -180,7 +178,10 @@ def tile_picked_tokhopnpagex_none_po_kernel(
             for t in range(PACK):
                 on_vector = PACK * (CHUNKS - 1 - c) + t >= N2_ON_SCALAR
                 gather(on_vector, den[:, t, :], st[t][:], entries(n2_t, cols.start, cols.stop))
-            invert(den)
+                if c == 0 and t % 2:
+                    invert(den[:, t - 1, :], den[:, t, :])
+            if c > 0:
+                invert(den[:, 0:2, :], den[:, 2:4, :])
             if c == 1:
                 gather(True, old[1][:], page[1][:], n3_t[:])
             z_bf = sb([P, CHUNK, PACK], BF16, "z_bf%d" % c)
@@ -188,6 +189,9 @@ def tile_picked_tokhopnpagex_none_po_kernel(
             z_q = sb([P, CHUNK], U32, "z_q%d" % c)
             z_s = sb([P, CHUNK], U8, "z_s%d" % c)
             nc.vector.quantize_mx(out=z_q[:].bitcast(FP8X4), scales=z_s[:], in_=z_bf[:].rearrange("p c t -> p (c t)"))
+            if c == 0:
+                old[0] = sb([P, H], F32, "old0", reuse="den0")
+                gather(False, old[0][:], page[0][:], n3_t[:])
             h_ps = psum.tile([P, 2, CHUNK], F32, name="h_ps%d" % c, tag="bank%d" % (PACK + c))
             h_early.append(h_ps)
             for t in range(PACK):
@@ -244,6 +248,6 @@ def tile_picked_tokhopnpagex_none_po_kernel(
             )
             nc.sync.dma_start(out=as_words(out_1)[:, out_cols(k)], in_=o_q[:].bitcast(I32))
         for q in range(QUADS):
-            nc.scalar.dma_start(
+            (nc.sync if q % 2 else nc.scalar).dma_start(
                 out=out_2[0, 4 * q : 4 * q + 4, :].bitcast(I32), in_=o_s[32 * q : 32 * q + 4, :].bitcast(I32)
             )

from contextlib import ExitStack

import concourse.mybir as mybir

K, T, S, N, H, U = 512, 2048, 512, 512, 512, 1024
FLOPS = 2 * S * K * H + 2 * N * S * H

F32 = mybir.dt.float32
BF16 = mybir.dt.bfloat16
I32 = mybir.dt.int32
U32 = mybir.dt.uint32
U16 = mybir.dt.uint16
U8 = mybir.dt.uint8
FP8X4 = mybir.dt.float8_e4m3fn_x4
ACT = mybir.ActivationFunctionType
ALU = mybir.AluOpType

P = 128
PACK = 4
QUADS = 4
HALF = H // 2
CHUNK = 128
CHUNKS = H // CHUNK
OUT_CHUNK = 256
OUT_CHUNKS = U // OUT_CHUNK
N1_ON_VECTOR = 2
N2_ON_SCALAR = 6


def tile_picked_tokhopnpagex_none_po_kernel(
    tc, x_words, x_scales, wa, gt, w1_words, w1_scales, mem, offs, n1, n2, n3, out_0, out_1, out_2
):
    nc = tc.nc
    with ExitStack() as ctx:
        keep = ctx.enter_context(tc.tile_pool(name="keep", bufs=1))
        psum = ctx.enter_context(tc.psum_pool(name="psum", bufs=1))

        def sb(shape, dtype, name, reuse=None):
            return keep.tile(shape, dtype, name=name, tag=reuse or name, align_bytes=64)

        def entries(list_tile, j0, j1):
            return list_tile[:, j0 // 16 : j1 // 16]

        def gather(on_vector, out, window, offsets):
            if on_vector:
                nc.vector.tensor_copy(out, window.indirect(offsets))
            else:
                nc.scalar.activation(out, window.indirect(offsets), ACT.Copy)

        def interleaved(ap):
            return ap.rearrange("p (c i) t -> p c t i", i=2)

        def by_tile(ap):
            return ap.rearrange("p t (c i) -> p c t i", i=2)

        def as_words(dram_bytes):
            return dram_bytes[0].rearrange("p n t -> p (n t)").bitcast(I32)

        def load_scale_rows(plane, dram_scales):
            for q in range(QUADS):
                nc.sync.dma_start(
                    out=plane[32 * q : 32 * q + 4, :].bitcast(I32), in_=dram_scales[0, 4 * q : 4 * q + 4, :].bitcast(I32)
                )

        offs_t = keep.tile([P, S // 16], U16, name="offs_t")
        n1_t = keep.tile([P, H // 16], U16, name="n1_t")
        n2_t = keep.tile([P, H // 16], U16, name="n2_t")
        n3_t = keep.tile([P, H // 16], U16, name="n3_t")
        wa_raw = sb([P, PACK, H], F32, "wa_raw")
        xw = sb([P, T], U32, "xw")
        xs = sb([P, T], U8, "xs")
        w1w = sb([P, N], U32, "w1w")
        w1s = sb([P, N], U8, "w1s")
        gt_t = sb([P, PACK], F32, "gt_t")
        page = [sb([P, U], F32, "page%d" % t) for t in range(PACK)]

        nc.gpsimd.memset(xs[:].bitcast(I32), 0)
        nc.gpsimd.memset(w1s[:].bitcast(I32), 0)
        warm = sb([P, 1], F32, "warm")
        nc.gpsimd.memset(warm[:], 1.0)
        nc.scalar.activation(warm[:], warm[:], ACT.Abs_reciprocal_sqrt)

        nc.sync.dma_start(out=wa_raw[:], in_=wa.rearrange("(p j) w -> p j w", j=PACK))
        load_scale_rows(xs, x_scales)
        nc.sync.dma_start(offs_t[:], offs)
        nc.sync.dma_start(out=xw[:].bitcast(I32), in_=as_words(x_words))
        nc.sync.dma_start(n1_t[:], n1)
        nc.sync.dma_start(out=w1w[:].bitcast(I32), in_=as_words(w1_words))
        load_scale_rows(w1s, w1_scales)
        nc.sync.dma_start(out=gt_t[:], in_=gt.rearrange("(p t) o -> p (t o)", t=PACK))
        nc.sync.dma_start(n2_t[:], n2)
        nc.sync.dma_start(n3_t[:], n3)
        mem_rows = mem.rearrange("(p t) u -> p t u", t=PACK)
        out_rows = out_0.rearrange("(p t) u -> p t u", t=PACK)
        for t in range(PACK):
            nc.sync.dma_start(out=page[t][:], in_=mem_rows[:, t, :])

        halves = (slice(0, HALF), slice(HALF, H))
        wa_bf = [sb([P, HALF, PACK], BF16, "wa_bf%d" % h) for h in range(2)]
        wa_q = sb([P, H], U32, "wa_q")
        wa_s = sb([P, H], U8, "wa_s")
        xs_picked = sb([P, PACK, P], U8, "xs_picked")
        xw_picked = sb([P, PACK, P], U32, "xw_picked")
        nc.vector.tensor_copy(xs_picked[:].rearrange("p t m -> p m t"), xs[:].indirect(offs_t[:]))
        nc.scalar.activation(interleaved(wa_bf[0][:]), by_tile(wa_raw[:, :, halves[0]]), ACT.Copy)
        nc.vector.tensor_copy(out=interleaved(wa_bf[1][:]), in_=by_tile(wa_raw[:, :, halves[1]]))
        for h in range(2):
            nc.vector.quantize_mx(
                out=wa_q[:, halves[h]].bitcast(FP8X4),
                scales=wa_s[:, halves[h]],
                in_=wa_bf[h][:].rearrange("p c t -> p (c t)"),
            )
        nc.vector.tensor_copy(xw_picked[:].rearrange("p t m -> p m t"), xw[:].indirect(offs_t[:]))

        w1w_dealt = sb([P, PACK, P], U32, "w1w_dealt")
        w1s_dealt = sb([P, PACK, P], U8, "w1s_dealt")
        nc.gpsimd.tensor_copy(out=w1w_dealt[:], in_=w1w[:].rearrange("p (m t) -> p t m", t=PACK))
        nc.gpsimd.tensor_copy(out=w1s_dealt[:], in_=w1s[:].rearrange("p (m t) -> p t m", t=PACK))

        y_ps = [psum.tile([P, H], F32, name="y_ps%d" % t, tag="bank%d" % t) for t in range(PACK)]
        for t in range(PACK):
            nc.tensor.matmul_mx(
                out=y_ps[t][:],
                lhsT=xw_picked[:, t, :].bitcast(FP8X4),
                lhsT_scale=xs_picked[:, t, :],
                rhs=wa_q[:].bitcast(FP8X4),
                rhs_scale=wa_s[:],
                start=True,
                stop=True,
            )

        y_sb = [sb([P, H], F32, "y_sb%d" % t) for t in range(PACK)]
        y_n1 = [sb([P, H], F32, "y_n1_%d" % t) for t in range(PACK)]
        st = [sb([P, H], F32, "st%d" % t) for t in range(PACK)]
        st_gt = sb([P, PACK, H], F32, "st_gt")

        def fetch_n1(t, h):
            cols = halves[h]
            gather(t < N1_ON_VECTOR, y_n1[t][:, cols], y_sb[t][:], entries(n1_t, cols.start, cols.stop))

        def subtract(t):
            nc.vector.tensor_tensor(st[t][:], y_ps[t][:], y_n1[t][:], ALU.subtract)
            nc.gpsimd.tensor_scalar(st_gt[:, t, :], st[t][:], gt_t[:, t : t + 1], 1.0, ALU.mult, ALU.mult)

        nc.vector.tensor_copy(y_sb[0][:], y_ps[0][:])
        for t in range(1, PACK):
            nc.scalar.copy(y_sb[t][:], y_ps[t][:])
        for t in range(PACK):
            fetch_n1(t, 0)
            if t > 0:
                subtract(t - 1)
            fetch_n1(t, 1)
        subtract(PACK - 1)
        old = {1: sb([P, H], F32, "old1", reuse="y_n1_3")}

        new_late = {t: sb([P, H], F32, "new_late%d" % t) for t in (2, 3)}
        h_late = {t: psum.tile([P, H], F32, name="h_late%d" % t, tag="bank%d" % (t - 2)) for t in (2, 3)}

        def invert(*parts):
            for v in parts:
                nc.scalar.activation(v, v, ACT.Abs)
            for v in parts:
                nc.scalar.activation(v, v, ACT.Abs_reciprocal_sqrt, bias=0.5)
            for v in parts:
                nc.scalar.activation(v, v, ACT.Square)

        def write_chunk(c, t, h_ps, reuse):
            cols = slice(c * CHUNK, (c + 1) * CHUNK)
            new = sb([P, CHUNK], F32, "new%d_%d" % (c, t), reuse=reuse)
            nc.vector.scalar_tensor_tensor(new[:], old[t][:, cols], 0.5, h_ps[:, t, :], ALU.mult, ALU.max)
            nc.vector.tensor_copy(page[t][:].indirect(entries(n3_t, cols.start, cols.stop)), new[:])

        den_buffer = ("den0", "y_n1_2", "y_n1_1", "z_bf0")
        h_early = []
        for c in range(CHUNKS):
            cols = slice(c * CHUNK, (c + 1) * CHUNK)
            den = sb([P, PACK, CHUNK], F32, "den%d" % c, reuse=den_buffer[c])
            for t in range(PACK):
                on_vector = PACK * (CHUNKS - 1 - c) + t >= N2_ON_SCALAR
                gather(on_vector, den[:, t, :], st[t][:], entries(n2_t, cols.start, cols.stop))
                if c == 0 and t % 2:
                    invert(den[:, t - 1, :], den[:, t, :])
            if c > 0:
                invert(den[:, 0:2, :], den[:, 2:4, :])
            if c == 1:
                gather(True, old[1][:], page[1][:], n3_t[:])
            z_bf = sb([P, CHUNK, PACK], BF16, "z_bf%d" % c)
            nc.vector.tensor_tensor(interleaved(z_bf[:]), by_tile(st_gt[:, :, cols]), by_tile(den[:]), ALU.mult)
            z_q = sb([P, CHUNK], U32, "z_q%d" % c)
            z_s = sb([P, CHUNK], U8, "z_s%d" % c)
            nc.vector.quantize_mx(out=z_q[:].bitcast(FP8X4), scales=z_s[:], in_=z_bf[:].rearrange("p c t -> p (c t)"))
            if c == 0:
                old[0] = sb([P, H], F32, "old0", reuse="den0")
                gather(False, old[0][:], page[0][:], n3_t[:])
            h_ps = psum.tile([P, 2, CHUNK], F32, name="h_ps%d" % c, tag="bank%d" % (PACK + c))
            h_early.append(h_ps)
            for t in range(PACK):
                nc.tensor.matmul_mx(
                    out=h_ps[:, t, :] if t < 2 else h_late[t][:, cols],
                    lhsT=w1w_dealt[:, t, :].bitcast(FP8X4),
                    lhsT_scale=w1s_dealt[:, t, :],
                    rhs=z_q[:].bitcast(FP8X4),
                    rhs_scale=z_s[:],
                    start=True,
                    stop=True,
                )
            if c > 0:
                write_chunk(c - 1, 1, h_early[c - 1], den_buffer[c])
            write_chunk(c, 0, h_ps, None)
        write_chunk(CHUNKS - 1, 1, h_early[CHUNKS - 1], None)

        early_bf = sb([P, 2, U], BF16, "early_bf")
        o_bf = [sb([P, OUT_CHUNK, PACK], BF16, "o_bf%d" % k) for k in range(OUT_CHUNKS)]
        o_s = sb([P, U], U8, "o_s")

        def out_cols(k):
            return slice(k * OUT_CHUNK, (k + 1) * OUT_CHUNK)

        for t in (2, 3):
            old_t = sb([P, H], F32, "old%d" % t, reuse="z_bf%d" % t)
            gather(False, old_t[:], page[t][:], n3_t[:])
            nc.vector.scalar_tensor_tensor(new_late[t][:], old_t[:], 0.5, h_late[t][:], ALU.mult, ALU.max)

        for t in (0, 1):
            nc.sync.dma_start(out=out_rows[:, t, :], in_=page[t][:])
            for h in range(2):
                cols = slice(h * (U // 2), (h + 1) * (U // 2))
                nc.scalar.copy(early_bf[:, t, cols], page[t][:, cols])
        for k in range(OUT_CHUNKS):
            nc.scalar.copy(out=o_bf[k][:, :, 0:2], in_=early_bf[:, :, out_cols(k)].rearrange("p t c -> p c t"))
        for t in (2, 3):
            nc.vector.tensor_copy(page[t][:].indirect(n3_t[:]), new_late[t][:])
            nc.sync.dma_start(out=out_rows[:, t, :], in_=page[t][:])
        late_bf = sb([P, 2, U // 2], BF16, "late_bf")
        nc.scalar.copy(late_bf[:, 0, :], page[2][:, U // 2 :])
        for t in (2, 3):
            for k in range(2):
                nc.scalar.copy(o_bf[k][:, :, t], page[t][:, out_cols(k)])
        for k in range(2):
            nc.vector.tensor_copy(late_bf[:, 1, out_cols(k)], page[3][:, out_cols(2 + k)])
        for k in range(2):
            nc.vector.tensor_copy(out=o_bf[2 + k][:, :, 2:4], in_=late_bf[:, :, out_cols(k)].rearrange("p t c -> p c t"))

        for k in (2, 3, 0, 1):
            o_q = sb([P, OUT_CHUNK], U32, "o_q%d" % k)
            nc.vector.quantize_mx(
                out=o_q[:].bitcast(FP8X4), scales=o_s[:, out_cols(k)], in_=o_bf[k][:].rearrange("p c t -> p (c t)")
            )
            nc.sync.dma_start(out=as_words(out_1)[:, out_cols(k)], in_=o_q[:].bitcast(I32))
        for q in range(QUADS):
            (nc.sync if q % 2 else nc.scalar).dma_start(
                out=out_2[0, 4 * q : 4 * q + 4, :].bitcast(I32), in_=o_s[32 * q : 32 * q + 4, :].bitcast(I32)
            )
